import numpy as np, ml_dtypes
CORES = [56,61,80,85]
N = 4
import mx_ref
NC, G = 512, 4
C = np.float32(0.037)
BF = ml_dtypes.bfloat16
def cut(t, i, w=512):
    return t[:, w * i:w * i + w]
def tile(rs):
    return np.stack(rs, axis=2).reshape(128, -1).astype(BF)
def layer(w, X):
    out = []
    for i in range(G):
        for t in range(len(X)):
            p = mx_ref.matmul(mx_ref.quantize(cut(w, len(X) * i + t)), X[t])
            z = p if t == 0 else z + p
        out.append(z)
    return out
def act(Z):
    return [np.maximum(z, 0) * C for z in Z]
def setup_inputs(rng):
    def f(*shape):
        return mx_ref.flush((rng.standard_normal(shape, dtype=np.float32) * np.exp2(rng.integers(-2, 3, shape[:-1] + (1,)))).astype(BF))
    return {"x": f(N, 128, 4 * NC), "w1": f(N, 128, G * 512), "w2": f(N, 128, 512)}
def setup_inputs_blocks(rng):
    d = setup_inputs(rng)
    for k in ("x", "w1", "w2"): d[k] = mx_ref.spread(d[k], rng, 2)
    return d
def setup_inputs_wide(rng):
    d = setup_inputs(rng)
    for k in ("x", "w1", "w2"): d[k] = mx_ref.flush((d[k].astype(np.float32) * np.exp2(rng.integers(-6, 7, (N, 1, 1))).astype(np.float32)).astype(BF))
    return d
def reference(x, w1, w2):
    X = [mx_ref.quantize(x[j]) for j in range(N)]
    y = np.zeros((N, 128, NC), np.float32)
    for c in range(N):
        for r in range(N):
            p = mx_ref.matmul(mx_ref.quantize(w2[r]), mx_ref.quantize(tile(act(layer(w1[r], [X[c]])))))
            y[c] = p if r == 0 else y[c] + p
    return {"y": y}

@@ -1,0 +1,218 @@
+from concourse.bass import DstId, RemoteDMATransfer
+from concourse.mybir import dt, AluOpType, ActivationFunctionType
+
+N = 4
+SIM_CORES = 96
+C = 0.037
+PK = 640
+W2C = 256
+HALF = ((0, 320), (320, 640))
+HT = 256
+NZ = 6
+
+SCRATCH = {
+    "w1b": ("sbuf", [128, 2048], "bfloat16"),
+    "w2b": ("sbuf", [128, 512], "bfloat16"),
+    "xb": ("sbuf", [128, 2048], "bfloat16"),
+    "xq": ("sbuf", [128, 512], "float8_e4m3fn_x4"),
+    "xs": ("sbuf", [128, 512], "uint8"),
+    "wq": ("sbuf", [128, N * PK], "float8_e4m3fn_x4"),
+    "ws": ("sbuf", [128, N * PK], "uint8"),
+    "h": ("sbuf", [128, 8 * 4 * HT], "bfloat16"),
+    "hq": ("sbuf", [128, 8 * HT], "float8_e4m3fn_x4"),
+    "hs": ("sbuf", [128, 8 * HT], "uint8"),
+    "yo": ("sbuf", [128, 512], "float32"),
+    "ps": ("psum", [128, 8 * 512], "float32"),
+}
+SEMAPHORES = (["l_w1a", "l_w1b", "l_w2", "l_xa", "l_xb", "q_w1a", "q_w1b", "q_w2", "q_xa", "q_xb",
+               "rc", "rs", "sent", "y0", "y1", "cp0", "cp1", "st0", "st1"]
+              + ["a%d%d" % (r, h) for r in range(N) for h in range(2)]
+              + ["z%d" % b for b in range(NZ)] + ["e%d" % b for b in range(NZ)] + ["hq%d" % u for u in range(8)])
+
+
+def tcol(t):
+    return 128 * t if t < 2 else 128 * (t + 1)
+
+
+def count(mask):
+    return bin(mask).count("1")
+
+
+def roads(T, topo):
+    cores = list(T.cores)
+    out = []
+    for s in cores:
+        near = [c for c in cores if c != s and topo.chip(c) == topo.chip(s)][0]
+        far = sorted([c for c in cores if topo.chip(c) != topo.chip(s)], key=lambda c: topo.die(c) != topo.die(s))
+
+        def helper(ch):
+            return [c for c in range(SIM_CORES)
+                    if topo.chip(c) == ch and c not in cores and topo.die(c) == topo.die(s)
+                    and all(topo.may_write(c, d) for d in far)][0]
+        chips = sorted(set(topo.chip(c) for c in range(SIM_CORES)))
+        mid = [m for m in chips if topo.same_plane(topo.chip(s), m) and topo.mates(m, topo.chip(far[0]))][0]
+        out.append({"core": s, "near": near, "far": far, "helper": (helper(mid), helper(topo.chip(s)))})
+    return out
+
+
+def views(T, r, h):
+    a, b = r * PK + HALF[h][0], r * PK + HALF[h][1]
+    return T.wq[:, a:b].bitcast(dt.uint8), T.ws[:, a:b]
+
+
+def transfer(topo, dst, mask, sem, ap):
+    rid, pid, _se = topo.addr(dst)
+    return RemoteDMATransfer(dst_ids=[DstId(rid=rid, pnc=pid)], dma_engine_mask=mask, remote_sem=sem, src=ap, dst=ap)
+
+
+def helper_program(g, core, T, topo, R):
+    for r in range(N):
+        for h in range(2):
+            if R[r]["helper"][h] != core:
+                continue
+            src = R[r]["core"]
+            n_in = count(topo.mask(src, core))
+            codes, plane = views(T, r, h)
+            sem = T.sem["a%d%d" % (r, h)]
+            sent = 0
+            first = True
+            for d in R[r]["far"]:
+                m = topo.mask(core, d)
+                if first:
+                    g.wait_ge(T.sem.rc, n_in)
+                g.remote_dma_fused([transfer(topo, d, m, sem, codes)], local_sem=T.sem.sent)
+                if first:
+                    g.wait_ge(T.sem.rs, n_in)
+                g.remote_dma_fused([transfer(topo, d, m, sem, plane)], local_sem=T.sem.sent)
+                sent += 2 * count(m)
+                first = False
+            g.wait_ge(T.sem.sent, sent)
+
+
+def rank_program(g, core, T, topo):
+    R = roads(T, topo)
+    rank = T.rank_of(core)
+    if rank is None:
+        helper_program(g, core, T, topo, R)
+        return
+    me = R[rank]
+    S = T.sem
+    te, ve, se, sy = g.tensor, g.vector, g.scalar, g.sync
+    lo = rank * PK
+
+    sy.dma_start(T.w1b[:, 0:1024], T.w1[:, 0:1024]).then_inc(S.l_w1a, 16)
+    se.dma_start(T.w2b[:], T.w2[:]).then_inc(S.l_w2, 16)
+    sy.dma_start(T.xb[:, 0:1024], T.x[:, 0:1024]).then_inc(S.l_xa, 16)
+    se.dma_start(T.w1b[:, 1024:2048], T.w1[:, 1024:2048]).then_inc(S.l_w1b, 16)
+    sy.dma_start(T.xb[:, 1024:2048], T.x[:, 1024:2048]).then_inc(S.l_xb, 16)
+
+    ve.wait_ge(S.l_w1a, 16)
+    ve.quantize_mx(T.wq[:, lo:lo + 256], T.ws[:, lo:lo + 256], T.w1b[:, 0:1024]).then_inc(S.q_w1a, 1)
+    ve.wait_ge(S.l_w2, 16)
+    ve.quantize_mx(T.wq[:, lo + W2C:lo + W2C + 128], T.ws[:, lo + W2C:lo + W2C + 128], T.w2b[:]).then_inc(S.q_w2, 1)
+    ve.wait_ge(S.l_xa, 16)
+    ve.quantize_mx(T.xq[:, 0:256], T.xs[:, 0:256], T.xb[:, 0:1024]).then_inc(S.q_xa, 1)
+    ve.wait_ge(S.l_w1b, 16)
+    ve.quantize_mx(T.wq[:, lo + 384:lo + 640], T.ws[:, lo + 384:lo + 640], T.w1b[:, 1024:2048]).then_inc(S.q_w1b, 1)
+    ve.wait_ge(S.l_xb, 16)
+    ve.quantize_mx(T.xq[:, 256:512], T.xs[:, 256:512], T.xb[:, 1024:2048]).then_inc(S.q_xb, 1)
+
+    hb, ha = me["helper"]
+    near = me["near"]
+    m_off = topo.mask(core, hb)
+    m_all = topo.mask(core, near)
+    m_rest = m_all & ~m_off
+    c0, p0 = views(T, rank, 0)
+    c1, p1 = views(T, rank, 1)
+    a0, a1 = S["a%d0" % rank], S["a%d1" % rank]
+    g.wait_ge(S.q_w1a, 1)
+    g.wait_ge(S.q_w2, 1)
+    g.remote_dma_fused([transfer(topo, hb, m_off, S.rc, c0), transfer(topo, near, m_rest, a0, c0)], local_sem=S.sent)
+    g.remote_dma_fused([transfer(topo, hb, m_off, S.rs, p0), transfer(topo, near, m_rest, a0, p0)], local_sem=S.sent)
+    g.wait_ge(S.q_w1b, 1)
+    m_ha = topo.mask(core, ha)
+    g.remote_dma_fused([transfer(topo, ha, m_ha, S.rc, c1)], local_sem=S.sent)
+    g.remote_dma_fused([transfer(topo, ha, m_ha, S.rs, p1)], local_sem=S.sent)
+    g.remote_dma_fused([transfer(topo, near, m_all, a1, c1)], local_sem=S.sent)
+    g.remote_dma_fused([transfer(topo, near, m_all, a1, p1)], local_sem=S.sent)
+    g.wait_ge(S.sent, 2 * (count(m_off) + count(m_rest)) + 2 * count(m_ha) + 2 * count(m_all))
+
+    def need(r, h):
+        if r == rank:
+            return [("q_w1a", 1), ("q_w2", 1)] if h == 0 else [("q_w1b", 1), ("q_w2", 1)]
+        o = R[r]
+        if o["near"] == core:
+            full = topo.mask(o["core"], core)
+            n = count(full & ~topo.mask(o["core"], o["helper"][0])) if h == 0 else count(full)
+        else:
+            n = count(topo.mask(o["helper"][h], core))
+        return [("a%d%d" % (r, h), 2 * n)]
+
+    seen = set()
+
+    def te_wait(pairs):
+        for p in pairs:
+            if p not in seen:
+                seen.add(p)
+                te.wait_ge(S[p[0]], p[1])
+
+    cores = list(T.cores)
+    order = [rank, cores.index(near)] + [cores.index(c) for c in me["far"]]
+    zn = [0]
+    unit_z = {}
+
+    def z_step(k, t, s):
+        r, u, z = order[k], 2 * k + s, zn[0]
+        zn[0] += 1
+        bank, use = z % NZ, z // NZ
+        w = r * PK + tcol(t)
+        te_wait(need(r, 0 if t < 2 else 1) + [("q_xb" if s else "q_xa", 1)])
+        if use:
+            te.wait_ge(S["e%d" % bank], use)
+        zp = T.ps[:, bank * 512:bank * 512 + HT]
+        te.matmul_mx(zp, T.wq[:, w:w + 128], T.ws[:, w:w + 128], T.xq[:, s * HT:(s + 1) * HT],
+                     T.xs[:, s * HT:(s + 1) * HT], True, True).then_inc(S["z%d" % bank], 1)
+        hv = T.h[:, u * 4 * HT + t:(u + 1) * 4 * HT:4]
+        if z % 2 == 0:
+            se.wait_ge(S["z%d" % bank], use + 1)
+            se.activation(hv, zp, ActivationFunctionType.Relu, scale=C).then_inc(S["e%d" % bank], 1)
+        else:
+            ve.wait_ge(S["z%d" % bank], use + 1)
+            ve.tensor_scalar(hv, zp, 0.0, C, AluOpType.max, AluOpType.mult).then_inc(S["e%d" % bank], 1)
+        unit_z.setdefault(u, []).append((bank, use + 1))
+        if len(unit_z[u]) == 4:
+            for b, n in unit_z[u]:
+                ve.wait_ge(S["e%d" % b], n)
+            ve.quantize_mx(T.hq[:, u * HT:(u + 1) * HT], T.hs[:, u * HT:(u + 1) * HT],
+                           T.h[:, u * 4 * HT:(u + 1) * 4 * HT]).then_inc(S["hq%d" % u], 1)
+
+    def y_step(k, s):
+        r, u = order[k], 2 * k + s
+        w = r * PK + W2C
+        te_wait(need(r, 0) + need(r, 1) + [("hq%d" % u, 1)])
+        te.matmul_mx(T.ps[:, (NZ + s) * 512:(NZ + s) * 512 + HT], T.wq[:, w:w + 128], T.ws[:, w:w + 128],
+                     T.hq[:, u * HT:(u + 1) * HT], T.hs[:, u * HT:(u + 1) * HT],
+                     k == 0, k == N - 1).then_inc(S["y%d" % s], 1)
+
+    for k in range(N):
+        if k == 0:
+            steps = [(t, s) for s in range(2) for t in range(4)]
+        else:
+            steps = [(0, 0), (1, 0), (0, 1), (1, 1), (2, 0), (3, 0), (2, 1), (3, 1)]
+        for i, (t, s) in enumerate(steps):
+            z_step(k, t, s)
+            if i == 1 and k > 0:
+                y_step(k - 1, 1)
+        y_step(k, 0)
+    y_step(N - 1, 1)
+
+    se.wait_ge(S.y0, N)
+    se.activation(T.yo[:, 0:HT], T.ps[:, NZ * 512:NZ * 512 + HT], ActivationFunctionType.Copy).then_inc(S.cp0, 1)
+    sy.wait_ge(S.cp0, 1)
+    sy.dma_start(T.y[:, 0:HT], T.yo[:, 0:HT]).then_inc(S.st0, 16)
+    ve.wait_ge(S.y1, N)
+    ve.tensor_copy(T.yo[:, HT:2 * HT], T.ps[:, (NZ + 1) * 512:(NZ + 1) * 512 + HT]).then_inc(S.cp1, 1)
+    se.wait_ge(S.cp1, 1)
+    se.dma_start(T.y[:, HT:2 * HT], T.yo[:, HT:2 * HT]).then_inc(S.st1, 16)
+    sy.wait_ge(S.st0, 16)
+    se.wait_ge(S.st1, 16)

@@ -6,7 +6,9 @@ SIM_CORES = 96
 C = 0.037
 PK = 640
 W2C = 256
-HALF = ((0, 320), (320, 640))
+W1P = ((0, 256), (384, 640))
+W2P = ((256, 320), (320, 384))
+NT = 512
 HT = 256
 NZ = 6
 
@@ -18,15 +20,15 @@ SCRATCH = {
     "xs": ("sbuf", [128, 512], "uint8"),
     "wq": ("sbuf", [128, N * PK], "float8_e4m3fn_x4"),
     "ws": ("sbuf", [128, N * PK], "uint8"),
-    "h": ("sbuf", [128, 8 * 4 * HT], "bfloat16"),
-    "hq": ("sbuf", [128, 8 * HT], "float8_e4m3fn_x4"),
-    "hs": ("sbuf", [128, 8 * HT], "uint8"),
+    "h": ("sbuf", [128, N * 4 * NT], "bfloat16"),
+    "hq": ("sbuf", [128, N * NT], "float8_e4m3fn_x4"),
+    "hs": ("sbuf", [128, N * NT], "uint8"),
     "yo": ("sbuf", [128, 512], "float32"),
     "ps": ("psum", [128, 8 * 512], "float32"),
 }
 SEMAPHORES = (["l_w1a", "l_w1b", "l_w2", "l_xa", "l_xb", "q_w1a", "q_w1b", "q_w2", "q_xa", "q_xb",
-               "rc", "rs", "sent", "y0", "y1", "cp0", "cp1", "st0", "st1"]
-              + ["a%d%d" % (r, h) for r in range(N) for h in range(2)]
+               "rc", "rs", "r2c", "r2s", "sent", "y0", "y1", "cp0", "cp1", "st0", "st1"]
+              + ["a%d%d" % (r, h) for r in range(N) for h in range(2)] + ["b%d" % r for r in range(N)]
               + ["z%d" % b for b in range(NZ)] + ["e%d" % b for b in range(NZ)] + ["hq%d" % u for u in range(8)])
 
 
@@ -36,6 +38,12 @@ def tcol(t):
 
 def count(mask):
     return bin(mask).count("1")
+
+
+def split(mask):
+    bits = [b for b in range(mask.bit_length()) if (mask >> b) & 1]
+    k = len(bits) // 2
+    return sum(1 << b for b in bits[:k]), sum(1 << b for b in bits[k:])
 
 
 def roads(T, topo):
@@ -55,8 +63,14 @@ def roads(T, topo):
     return out
 
 
-def views(T, r, h):
-    a, b = r * PK + HALF[h][0], r * PK + HALF[h][1]
+def masks_out(topo, o):
+    m_off = topo.mask(o["core"], o["helper"][0])
+    m_all = topo.mask(o["core"], o["near"])
+    return m_off, m_all & ~m_off, m_all
+
+
+def views(T, r, cols):
+    a, b = r * PK + cols[0], r * PK + cols[1]
     return T.wq[:, a:b].bitcast(dt.uint8), T.ws[:, a:b]
 
 
@@ -66,27 +80,31 @@ def transfer(topo, dst, mask, sem, ap):
 
 
 def helper_program(g, core, T, topo, R):
+    S = T.sem
     for r in range(N):
         for h in range(2):
             if R[r]["helper"][h] != core:
                 continue
-            src = R[r]["core"]
-            n_in = count(topo.mask(src, core))
-            codes, plane = views(T, r, h)
-            sem = T.sem["a%d%d" % (r, h)]
-            sent = 0
-            first = True
-            for d in R[r]["far"]:
-                m = topo.mask(core, d)
-                if first:
-                    g.wait_ge(T.sem.rc, n_in)
-                g.remote_dma_fused([transfer(topo, d, m, sem, codes)], local_sem=T.sem.sent)
-                if first:
-                    g.wait_ge(T.sem.rs, n_in)
-                g.remote_dma_fused([transfer(topo, d, m, sem, plane)], local_sem=T.sem.sent)
-                sent += 2 * count(m)
-                first = False
-            g.wait_ge(T.sem.sent, sent)
+            m_off, m_rest, _m_all = masks_out(topo, R[r])
+            n2 = count(m_off if h == 0 else m_rest)
+            n1 = count(topo.mask(R[r]["core"], core))
+            f0, f1 = R[r]["far"]
+            m = topo.mask(core, f0)
+            ma, mb = split(m)
+            c2, p2 = views(T, r, W2P[h])
+            c1, p1 = views(T, r, W1P[h])
+            sa, sb = S["a%d%d" % (r, h)], S["b%d" % r]
+            g.wait_ge(S.r2s, n2)
+            g.remote_dma_fused([transfer(topo, f0, ma, sb, p2), transfer(topo, f1, mb, sb, p2)], local_sem=S.sent)
+            g.wait_ge(S.r2c, n2)
+            g.remote_dma_fused([transfer(topo, f0, ma, sb, c2), transfer(topo, f1, mb, sb, c2)], local_sem=S.sent)
+            g.wait_ge(S.rs, n1)
+            g.remote_dma_fused([transfer(topo, f0, m, sa, p1)], local_sem=S.sent)
+            g.wait_ge(S.rc, n1)
+            g.remote_dma_fused([transfer(topo, f0, m, sa, c1)], local_sem=S.sent)
+            g.remote_dma_fused([transfer(topo, f1, m, sa, p1)], local_sem=S.sent)
+            g.remote_dma_fused([transfer(topo, f1, m, sa, c1)], local_sem=S.sent)
+            g.wait_ge(S.sent, 2 * (count(ma) + count(mb)) + 4 * count(m))
 
 
 def rank_program(g, core, T, topo):
@@ -100,16 +118,16 @@ def rank_program(g, core, T, topo):
     te, ve, se, sy = g.tensor, g.vector, g.scalar, g.sync
     lo = rank * PK
 
-    sy.dma_start(T.w1b[:, 0:1024], T.w1[:, 0:1024]).then_inc(S.l_w1a, 16)
     se.dma_start(T.w2b[:], T.w2[:]).then_inc(S.l_w2, 16)
+    sy.dma_start(T.w1b[:, 0:1024], T.w1[:, 0:1024]).then_inc(S.l_w1a, 16)
     sy.dma_start(T.xb[:, 0:1024], T.x[:, 0:1024]).then_inc(S.l_xa, 16)
     se.dma_start(T.w1b[:, 1024:2048], T.w1[:, 1024:2048]).then_inc(S.l_w1b, 16)
     sy.dma_start(T.xb[:, 1024:2048], T.x[:, 1024:2048]).then_inc(S.l_xb, 16)
 
-    ve.wait_ge(S.l_w1a, 16)
-    ve.quantize_mx(T.wq[:, lo:lo + 256], T.ws[:, lo:lo + 256], T.w1b[:, 0:1024]).then_inc(S.q_w1a, 1)
     ve.wait_ge(S.l_w2, 16)
     ve.quantize_mx(T.wq[:, lo + W2C:lo + W2C + 128], T.ws[:, lo + W2C:lo + W2C + 128], T.w2b[:]).then_inc(S.q_w2, 1)
+    ve.wait_ge(S.l_w1a, 16)
+    ve.quantize_mx(T.wq[:, lo:lo + 256], T.ws[:, lo:lo + 256], T.w1b[:, 0:1024]).then_inc(S.q_w1a, 1)
     ve.wait_ge(S.l_xa, 16)
     ve.quantize_mx(T.xq[:, 0:256], T.xs[:, 0:256], T.xb[:, 0:1024]).then_inc(S.q_xa, 1)
     ve.wait_ge(S.l_w1b, 16)
@@ -119,34 +137,38 @@ def rank_program(g, core, T, topo):
 
     hb, ha = me["helper"]
     near = me["near"]
-    m_off = topo.mask(core, hb)
-    m_all = topo.mask(core, near)
-    m_rest = m_all & ~m_off
-    c0, p0 = views(T, rank, 0)
-    c1, p1 = views(T, rank, 1)
-    a0, a1 = S["a%d0" % rank], S["a%d1" % rank]
-    g.wait_ge(S.q_w1a, 1)
-    g.wait_ge(S.q_w2, 1)
-    g.remote_dma_fused([transfer(topo, hb, m_off, S.rc, c0), transfer(topo, near, m_rest, a0, c0)], local_sem=S.sent)
-    g.remote_dma_fused([transfer(topo, hb, m_off, S.rs, p0), transfer(topo, near, m_rest, a0, p0)], local_sem=S.sent)
-    g.wait_ge(S.q_w1b, 1)
+    m_off, m_rest, m_all = masks_out(topo, me)
     m_ha = topo.mask(core, ha)
-    g.remote_dma_fused([transfer(topo, ha, m_ha, S.rc, c1)], local_sem=S.sent)
-    g.remote_dma_fused([transfer(topo, ha, m_ha, S.rs, p1)], local_sem=S.sent)
-    g.remote_dma_fused([transfer(topo, near, m_all, a1, c1)], local_sem=S.sent)
-    g.remote_dma_fused([transfer(topo, near, m_all, a1, p1)], local_sem=S.sent)
-    g.wait_ge(S.sent, 2 * (count(m_off) + count(m_rest)) + 2 * count(m_ha) + 2 * count(m_all))
+    c2a, p2a = views(T, rank, W2P[0])
+    c2b, p2b = views(T, rank, W2P[1])
+    c1a, p1a = views(T, rank, W1P[0])
+    c1b, p1b = views(T, rank, W1P[1])
+    cn, pn = views(T, rank, (W2C, PK))
+    a0, a1 = S["a%d0" % rank], S["a%d1" % rank]
+    g.wait_ge(S.q_w2, 1)
+    g.remote_dma_fused([transfer(topo, hb, m_off, S.r2s, p2a), transfer(topo, ha, m_rest, S.r2s, p2b)], local_sem=S.sent)
+    g.remote_dma_fused([transfer(topo, hb, m_off, S.r2c, c2a), transfer(topo, ha, m_rest, S.r2c, c2b)], local_sem=S.sent)
+    g.wait_ge(S.q_w1a, 1)
+    g.remote_dma_fused([transfer(topo, hb, m_off, S.rs, p1a), transfer(topo, near, m_rest, a0, p1a)], local_sem=S.sent)
+    g.remote_dma_fused([transfer(topo, hb, m_off, S.rc, c1a), transfer(topo, near, m_rest, a0, c1a)], local_sem=S.sent)
+    g.wait_ge(S.q_w1b, 1)
+    g.remote_dma_fused([transfer(topo, ha, m_ha, S.rs, p1b)], local_sem=S.sent)
+    g.remote_dma_fused([transfer(topo, ha, m_ha, S.rc, c1b)], local_sem=S.sent)
+    g.remote_dma_fused([transfer(topo, near, m_all, a1, pn)], local_sem=S.sent)
+    g.remote_dma_fused([transfer(topo, near, m_all, a1, cn)], local_sem=S.sent)
+    g.wait_ge(S.sent, 4 * (count(m_off) + count(m_rest)) + 2 * count(m_ha) + 2 * count(m_all))
 
-    def need(r, h):
+    def need(r, part):
         if r == rank:
-            return [("q_w1a", 1), ("q_w2", 1)] if h == 0 else [("q_w1b", 1), ("q_w2", 1)]
+            return [(("q_w1a", "q_w1b", "q_w2")[part], 1)]
         o = R[r]
         if o["near"] == core:
-            full = topo.mask(o["core"], core)
-            n = count(full & ~topo.mask(o["core"], o["helper"][0])) if h == 0 else count(full)
-        else:
-            n = count(topo.mask(o["helper"][h], core))
-        return [("a%d%d" % (r, h), 2 * n)]
+            _off, rest, full = masks_out(topo, o)
+            return [("a%d0" % r, 2 * count(rest))] if part == 0 else [("a%d1" % r, 2 * count(full))]
+        if part < 2:
+            return [("a%d%d" % (r, part), 2 * count(topo.mask(o["helper"][part], core)))]
+        i = o["far"].index(core)
+        return [("b%d" % r, sum(2 * count(split(topo.mask(hc, core))[i]) for hc in o["helper"]))]
 
     seen = set()
 
@@ -160,51 +182,68 @@ def rank_program(g, core, T, topo):
     order = [rank, cores.index(near)] + [cores.index(c) for c in me["far"]]
     zn = [0]
     unit_z = {}
+    yn = [0, 0]
 
-    def z_step(k, t, s):
-        r, u, z = order[k], 2 * k + s, zn[0]
+    def z_step(k, t, halves, on_scalar):
+        r, z = order[k], zn[0]
         zn[0] += 1
         bank, use = z % NZ, z // NZ
         w = r * PK + tcol(t)
-        te_wait(need(r, 0 if t < 2 else 1) + [("q_xb" if s else "q_xa", 1)])
+        c0, c1 = halves[0] * HT, (halves[-1] + 1) * HT
+        te_wait(need(r, 0 if t < 2 else 1) + [("q_xb" if s else "q_xa", 1) for s in halves])
         if use:
             te.wait_ge(S["e%d" % bank], use)
-        zp = T.ps[:, bank * 512:bank * 512 + HT]
-        te.matmul_mx(zp, T.wq[:, w:w + 128], T.ws[:, w:w + 128], T.xq[:, s * HT:(s + 1) * HT],
-                     T.xs[:, s * HT:(s + 1) * HT], True, True).then_inc(S["z%d" % bank], 1)
-        hv = T.h[:, u * 4 * HT + t:(u + 1) * 4 * HT:4]
-        if z % 2 == 0:
+        zp = T.ps[:, bank * 512:bank * 512 + c1 - c0]
+        te.matmul_mx(zp, T.wq[:, w:w + 128], T.ws[:, w:w + 128], T.xq[:, c0:c1], T.xs[:, c0:c1],
+                     True, True).then_inc(S["z%d" % bank], 1)
+        hv = T.h[:, 4 * (k * NT + c0) + t:4 * (k * NT + c1):4]
+        if on_scalar:
             se.wait_ge(S["z%d" % bank], use + 1)
             se.activation(hv, zp, ActivationFunctionType.Relu, scale=C).then_inc(S["e%d" % bank], 1)
         else:
             ve.wait_ge(S["z%d" % bank], use + 1)
             ve.tensor_scalar(hv, zp, 0.0, C, AluOpType.max, AluOpType.mult).then_inc(S["e%d" % bank], 1)
-        unit_z.setdefault(u, []).append((bank, use + 1))
-        if len(unit_z[u]) == 4:
-            for b, n in unit_z[u]:
-                ve.wait_ge(S["e%d" % b], n)
-            ve.quantize_mx(T.hq[:, u * HT:(u + 1) * HT], T.hs[:, u * HT:(u + 1) * HT],
-                           T.h[:, u * 4 * HT:(u + 1) * 4 * HT]).then_inc(S["hq%d" % u], 1)
+        for s in halves:
+            u = 2 * k + s
+            unit_z.setdefault(u, []).append((bank, use + 1))
+            if len(unit_z[u]) == 4:
+                for b, n in unit_z[u]:
+                    ve.wait_ge(S["e%d" % b], n)
+                ve.quantize_mx(T.hq[:, u * HT:(u + 1) * HT], T.hs[:, u * HT:(u + 1) * HT],
+                               T.h[:, u * 4 * HT:(u + 1) * 4 * HT]).then_inc(S["hq%d" % u], 1)
 
     def y_step(k, s):
         r, u = order[k], 2 * k + s
         w = r * PK + W2C
-        te_wait(need(r, 0) + need(r, 1) + [("hq%d" % u, 1)])
+        te_wait(need(r, 2) + [("hq%d" % u, 1)])
+        yn[s] += 1
         te.matmul_mx(T.ps[:, (NZ + s) * 512:(NZ + s) * 512 + HT], T.wq[:, w:w + 128], T.ws[:, w:w + 128],
                      T.hq[:, u * HT:(u + 1) * HT], T.hs[:, u * HT:(u + 1) * HT],
-                     k == 0, k == N - 1).then_inc(S["y%d" % s], 1)
+                     yn[s] == 1, yn[s] == N).then_inc(S["y%d" % s], 1)
 
-    for k in range(N):
-        if k == 0:
-            steps = [(t, s) for s in range(2) for t in range(4)]
-        else:
-            steps = [(0, 0), (1, 0), (0, 1), (1, 1), (2, 0), (3, 0), (2, 1), (3, 1)]
-        for i, (t, s) in enumerate(steps):
-            z_step(k, t, s)
-            if i == 1 and k > 0:
-                y_step(k - 1, 1)
-        y_step(k, 0)
-    y_step(N - 1, 1)
+    def owner(k, after_first_part=()):
+        z_step(k, 0, (0, 1), True)
+        z_step(k, 1, (0, 1), False)
+        for kk, s in after_first_part:
+            y_step(kk, s)
+        z_step(k, 2, (0, 1), True)
+        z_step(k, 3, (0,), False)
+        z_step(k, 3, (1,), True)
+
+    for t in range(4):
+        z_step(0, t, (0,), True)
+    for t in range(4):
+        z_step(0, t, (1,), t % 2 == 1)
+    owner(1)
+    y_step(0, 0)
+    y_step(0, 1)
+    y_step(1, 0)
+    owner(2, after_first_part=[(1, 1)])
+    owner(3)
+    y_step(2, 0)
+    y_step(2, 1)
+    y_step(3, 0)
+    y_step(3, 1)
 
     se.wait_ge(S.y0, N)
     se.activation(T.yo[:, 0:HT], T.ps[:, NZ * 512:NZ * 512 + HT], ActivationFunctionType.Copy).then_inc(S.cp0, 1)

@@ -27,8 +27,10 @@ SCRATCH = {
     "ps": ("psum", [128, 8 * 512], "float32"),
 }
 SEMAPHORES = (["l_w1a", "l_w1b", "l_w2", "l_xa", "l_xb", "q_w1a", "q_w1b", "q_w2", "q_xa", "q_xb",
-               "rc", "rs", "r2c", "r2s", "sent", "y0", "y1", "cp0", "cp1", "st0", "st1"]
-              + ["a%d%d" % (r, h) for r in range(N) for h in range(2)] + ["b%d" % r for r in range(N)]
+               "rc0", "rc1", "rs", "r2c", "r2s", "sent", "y0", "y1", "cp0", "cp1", "st0", "st1"]
+              + ["a%d%d" % (r, t) for r in range(N) for t in range(4)]
+              + ["p%d%d" % (r, h) for r in range(N) for h in range(2)]
+              + ["b%d" % r for r in range(N)]
               + ["z%d" % b for b in range(NZ)] + ["e%d" % b for b in range(NZ)] + ["hq%d" % u for u in range(8)])
 
 
@@ -74,6 +76,10 @@ def views(T, r, cols):
     return T.wq[:, a:b].bitcast(dt.uint8), T.ws[:, a:b]
 
 
+def tile_codes(T, r, t):
+    return views(T, r, (tcol(t), tcol(t) + 128))[0]
+
+
 def transfer(topo, dst, mask, sem, ap):
     rid, pid, _se = topo.addr(dst)
     return RemoteDMATransfer(dst_ids=[DstId(rid=rid, pnc=pid)], dma_engine_mask=mask, remote_sem=sem, src=ap, dst=ap)
@@ -86,25 +92,29 @@ def helper_program(g, core, T, topo, R):
             if R[r]["helper"][h] != core:
                 continue
             m_off, m_rest, _m_all = masks_out(topo, R[r])
-            n2 = count(m_off if h == 0 else m_rest)
-            n1 = count(topo.mask(R[r]["core"], core))
+            n1 = count(m_off if h == 0 else m_rest)
+            n2s = count(m_off if h == 0 else split(m_rest)[0])
+            n2c = count(split(m_off if h == 0 else m_rest)[0])
             f0, f1 = R[r]["far"]
             m = topo.mask(core, f0)
             ma, mb = split(m)
             c2, p2 = views(T, r, W2P[h])
-            c1, p1 = views(T, r, W1P[h])
-            sa, sb = S["a%d%d" % (r, h)], S["b%d" % r]
-            g.wait_ge(S.r2s, n2)
+            p1 = views(T, r, W1P[h])[1]
+            t0, t1 = 2 * h, 2 * h + 1
+            sp, sb = S["p%d%d" % (r, h)], S["b%d" % r]
+            g.wait_ge(S.r2s, n2s)
             g.remote_dma_fused([transfer(topo, f0, ma, sb, p2), transfer(topo, f1, mb, sb, p2)], local_sem=S.sent)
-            g.wait_ge(S.r2c, n2)
-            g.remote_dma_fused([transfer(topo, f0, ma, sb, c2), transfer(topo, f1, mb, sb, c2)], local_sem=S.sent)
             g.wait_ge(S.rs, n1)
-            g.remote_dma_fused([transfer(topo, f0, m, sa, p1)], local_sem=S.sent)
-            g.wait_ge(S.rc, n1)
-            g.remote_dma_fused([transfer(topo, f0, m, sa, c1)], local_sem=S.sent)
-            g.remote_dma_fused([transfer(topo, f1, m, sa, p1)], local_sem=S.sent)
-            g.remote_dma_fused([transfer(topo, f1, m, sa, c1)], local_sem=S.sent)
-            g.wait_ge(S.sent, 2 * (count(ma) + count(mb)) + 4 * count(m))
+            g.remote_dma_fused([transfer(topo, f0, ma, sp, p1), transfer(topo, f1, mb, sp, p1)], local_sem=S.sent)
+            g.wait_ge(S.rc0, n1)
+            g.remote_dma_fused([transfer(topo, f0, m, S["a%d%d" % (r, t0)], tile_codes(T, r, t0))], local_sem=S.sent)
+            g.wait_ge(S.rc1, n1)
+            g.remote_dma_fused([transfer(topo, f0, m, S["a%d%d" % (r, t1)], tile_codes(T, r, t1))], local_sem=S.sent)
+            g.remote_dma_fused([transfer(topo, f1, m, S["a%d%d" % (r, t0)], tile_codes(T, r, t0))], local_sem=S.sent)
+            g.remote_dma_fused([transfer(topo, f1, m, S["a%d%d" % (r, t1)], tile_codes(T, r, t1))], local_sem=S.sent)
+            g.wait_ge(S.r2c, n2c)
+            g.remote_dma_fused([transfer(topo, f0, ma, sb, c2), transfer(topo, f1, mb, sb, c2)], local_sem=S.sent)
+            g.wait_ge(S.sent, 3 * (count(ma) + count(mb)) + 4 * count(m))
 
 
 def rank_program(g, core, T, topo):
@@ -137,37 +147,52 @@ def rank_program(g, core, T, topo):
 
     hb, ha = me["helper"]
     near = me["near"]
-    m_off, m_rest, m_all = masks_out(topo, me)
-    m_ha = topo.mask(core, ha)
+    m_off, m_rest, _m_all = masks_out(topo, me)
+    oa, ob = split(m_off)
+    ra, rb = split(m_rest)
     c2a, p2a = views(T, rank, W2P[0])
     c2b, p2b = views(T, rank, W2P[1])
-    c1a, p1a = views(T, rank, W1P[0])
-    c1b, p1b = views(T, rank, W1P[1])
-    cn, pn = views(T, rank, (W2C, PK))
-    a0, a1 = S["a%d0" % rank], S["a%d1" % rank]
-    g.wait_ge(S.q_w2, 1)
-    g.remote_dma_fused([transfer(topo, hb, m_off, S.r2s, p2a), transfer(topo, ha, m_rest, S.r2s, p2b)], local_sem=S.sent)
-    g.remote_dma_fused([transfer(topo, hb, m_off, S.r2c, c2a), transfer(topo, ha, m_rest, S.r2c, c2b)], local_sem=S.sent)
-    g.wait_ge(S.q_w1a, 1)
-    g.remote_dma_fused([transfer(topo, hb, m_off, S.rs, p1a), transfer(topo, near, m_rest, a0, p1a)], local_sem=S.sent)
-    g.remote_dma_fused([transfer(topo, hb, m_off, S.rc, c1a), transfer(topo, near, m_rest, a0, c1a)], local_sem=S.sent)
-    g.wait_ge(S.q_w1b, 1)
-    g.remote_dma_fused([transfer(topo, ha, m_ha, S.rs, p1b)], local_sem=S.sent)
-    g.remote_dma_fused([transfer(topo, ha, m_ha, S.rc, c1b)], local_sem=S.sent)
-    g.remote_dma_fused([transfer(topo, near, m_all, a1, pn)], local_sem=S.sent)
-    g.remote_dma_fused([transfer(topo, near, m_all, a1, cn)], local_sem=S.sent)
-    g.wait_ge(S.sent, 4 * (count(m_off) + count(m_rest)) + 2 * count(m_ha) + 2 * count(m_all))
+    p1a = views(T, rank, W1P[0])[1]
+    p1b = views(T, rank, W1P[1])[1]
+    b2 = S["b%d" % rank]
 
-    def need(r, part):
+    def send_tile(t, hc, m_h, m_n):
+        cc = tile_codes(T, rank, t)
+        g.remote_dma_fused([transfer(topo, hc, m_h, S["rc%d" % (t % 2)], cc),
+                            transfer(topo, near, m_n, S["a%d%d" % (rank, t)], cc)], local_sem=S.sent)
+
+    g.wait_ge(S.q_w2, 1)
+    g.remote_dma_fused([transfer(topo, hb, m_off, S.r2s, p2a), transfer(topo, ha, ra, S.r2s, p2b)], local_sem=S.sent)
+    g.wait_ge(S.q_w1a, 1)
+    g.remote_dma_fused([transfer(topo, hb, m_off, S.rs, p1a),
+                        transfer(topo, near, m_rest, S["p%d0" % rank], p1a)], local_sem=S.sent)
+    send_tile(0, hb, m_off, m_rest)
+    send_tile(1, hb, m_off, m_rest)
+    g.wait_ge(S.q_w1b, 1)
+    g.remote_dma_fused([transfer(topo, ha, m_rest, S.rs, p1b),
+                        transfer(topo, near, m_off, S["p%d1" % rank], p1b)], local_sem=S.sent)
+    send_tile(2, ha, m_rest, m_off)
+    send_tile(3, ha, m_rest, m_off)
+    g.remote_dma_fused([transfer(topo, hb, oa, S.r2c, c2a), transfer(topo, ha, ra, S.r2c, c2b),
+                        transfer(topo, near, ob, b2, c2a), transfer(topo, near, rb, b2, c2b)], local_sem=S.sent)
+    g.remote_dma_fused([transfer(topo, near, ra, b2, p2a), transfer(topo, near, rb, b2, p2b)], local_sem=S.sent)
+    g.wait_ge(S.sent, count(m_off) + count(ra) + 7 * (count(m_off) + count(m_rest)) + count(m_rest))
+
+    def need(r, t):
+        part = t // 2
         if r == rank:
             return [(("q_w1a", "q_w1b", "q_w2")[part], 1)]
         o = R[r]
         if o["near"] == core:
-            _off, rest, full = masks_out(topo, o)
-            return [("a%d0" % r, 2 * count(rest))] if part == 0 else [("a%d1" % r, 2 * count(full))]
-        if part < 2:
-            return [("a%d%d" % (r, part), 2 * count(topo.mask(o["helper"][part], core)))]
+            off, rest, _full = masks_out(topo, o)
+            if part == 2:
+                return [("b%d" % r, count(split(off)[1]) + count(split(rest)[1]) + count(rest))]
+            n = count(rest if part == 0 else off)
+            return [("p%d%d" % (r, part), n), ("a%d%d" % (r, t), n)]
         i = o["far"].index(core)
+        if part < 2:
+            mh = topo.mask(o["helper"][part], core)
+            return [("p%d%d" % (r, part), count(split(mh)[i])), ("a%d%d" % (r, t), count(mh))]
         return [("b%d" % r, sum(2 * count(split(topo.mask(hc, core))[i]) for hc in o["helper"]))]
 
     seen = set()
@@ -190,7 +215,7 @@ def rank_program(g, core, T, topo):
         bank, use = z % NZ, z // NZ
         w = r * PK + tcol(t)
         c0, c1 = halves[0] * HT, (halves[-1] + 1) * HT
-        te_wait(need(r, 0 if t < 2 else 1) + [("q_xb" if s else "q_xa", 1) for s in halves])
+        te_wait(need(r, t) + [("q_xb" if s else "q_xa", 1) for s in halves])
         if use:
             te.wait_ge(S["e%d" % bank], use)
         zp = T.ps[:, bank * 512:bank * 512 + c1 - c0]
@@ -215,31 +240,31 @@ def rank_program(g, core, T, topo):
     def y_step(k, s):
         r, u = order[k], 2 * k + s
         w = r * PK + W2C
-        te_wait(need(r, 2) + [("hq%d" % u, 1)])
+        te_wait(need(r, 4) + [("hq%d" % u, 1)])
         yn[s] += 1
         te.matmul_mx(T.ps[:, (NZ + s) * 512:(NZ + s) * 512 + HT], T.wq[:, w:w + 128], T.ws[:, w:w + 128],
                      T.hq[:, u * HT:(u + 1) * HT], T.hs[:, u * HT:(u + 1) * HT],
                      yn[s] == 1, yn[s] == N).then_inc(S["y%d" % s], 1)
 
-    def owner(k, after_first_part=()):
-        z_step(k, 0, (0, 1), True)
-        z_step(k, 1, (0, 1), False)
-        for kk, s in after_first_part:
+    def owner(k, tiles, after_two=()):
+        z_step(k, tiles[0], (0, 1), True)
+        z_step(k, tiles[1], (0, 1), False)
+        for kk, s in after_two:
             y_step(kk, s)
-        z_step(k, 2, (0, 1), True)
-        z_step(k, 3, (0,), False)
-        z_step(k, 3, (1,), True)
+        z_step(k, tiles[2], (0, 1), True)
+        z_step(k, tiles[3], (0,), False)
+        z_step(k, tiles[3], (1,), True)
 
     for t in range(4):
         z_step(0, t, (0,), True)
     for t in range(4):
         z_step(0, t, (1,), t % 2 == 1)
-    owner(1)
+    owner(1, (0, 1, 2, 3))
     y_step(0, 0)
     y_step(0, 1)
     y_step(1, 0)
-    owner(2, after_first_part=[(1, 1)])
-    owner(3)
+    owner(2, (0, 2, 1, 3), after_two=[(1, 1)])
+    owner(3, (0, 2, 1, 3))
     y_step(2, 0)
     y_step(2, 1)
     y_step(3, 0)

from concourse.bass import DstId, RemoteDMATransfer
from concourse.mybir import dt, AluOpType, ActivationFunctionType

N = 4
SIM_CORES = 96
C = 0.037
PK = 640
W2C = 256
W1P = ((0, 256), (384, 640))
W2P = ((256, 320), (320, 384))
NT = 512
HT = 256
NZ = 6

SCRATCH = {
    "w1b": ("sbuf", [128, 2048], "bfloat16"),
    "w2b": ("sbuf", [128, 512], "bfloat16"),
    "xb": ("sbuf", [128, 2048], "bfloat16"),
    "xq": ("sbuf", [128, 512], "float8_e4m3fn_x4"),
    "xs": ("sbuf", [128, 512], "uint8"),
    "wq": ("sbuf", [128, N * PK], "float8_e4m3fn_x4"),
    "ws": ("sbuf", [128, N * PK], "uint8"),
    "h": ("sbuf", [128, N * 4 * NT], "bfloat16"),
    "hq": ("sbuf", [128, N * NT], "float8_e4m3fn_x4"),
    "hs": ("sbuf", [128, N * NT], "uint8"),
    "yo": ("sbuf", [128, 512], "float32"),
    "ps": ("psum", [128, 8 * 512], "float32"),
}
SEMAPHORES = (["l_w1a", "l_w1b", "l_w2", "l_xa", "l_xb", "q_w1a", "q_w1b", "q_w2", "q_xa", "q_xb",
               "rc0", "rc1", "rs", "r2c", "r2s", "sent", "y0", "y1", "cp0", "cp1", "st0", "st1"]
              + ["a%d%d" % (r, t) for r in range(N) for t in range(4)]
              + ["p%d%d" % (r, h) for r in range(N) for h in range(2)]
              + ["b%d" % r for r in range(N)]
              + ["z%d" % b for b in range(NZ)] + ["e%d" % b for b in range(NZ)] + ["hq%d" % u for u in range(8)])


def tcol(t):
    return 128 * t if t < 2 else 128 * (t + 1)


def count(mask):
    return bin(mask).count("1")


def split(mask):
    bits = [b for b in range(mask.bit_length()) if (mask >> b) & 1]
    k = len(bits) // 2
    return sum(1 << b for b in bits[:k]), sum(1 << b for b in bits[k:])


def roads(T, topo):
    cores = list(T.cores)
    out = []
    for s in cores:
        near = [c for c in cores if c != s and topo.chip(c) == topo.chip(s)][0]
        far = sorted([c for c in cores if topo.chip(c) != topo.chip(s)], key=lambda c: topo.die(c) != topo.die(s))

        def helper(ch):
            return [c for c in range(SIM_CORES)
                    if topo.chip(c) == ch and c not in cores and topo.die(c) == topo.die(s)
                    and all(topo.may_write(c, d) for d in far)][0]
        chips = sorted(set(topo.chip(c) for c in range(SIM_CORES)))
        mid = [m for m in chips if topo.same_plane(topo.chip(s), m) and topo.mates(m, topo.chip(far[0]))][0]
        out.append({"core": s, "near": near, "far": far, "helper": (helper(mid), helper(topo.chip(s)))})
    return out


def masks_out(topo, o):
    m_off = topo.mask(o["core"], o["helper"][0])
    m_all = topo.mask(o["core"], o["near"])
    return m_off, m_all & ~m_off, m_all


def views(T, r, cols):
    a, b = r * PK + cols[0], r * PK + cols[1]
    return T.wq[:, a:b].bitcast(dt.uint8), T.ws[:, a:b]


def tile_codes(T, r, t):
    return views(T, r, (tcol(t), tcol(t) + 128))[0]


def transfer(topo, dst, mask, sem, ap):
    rid, pid, _se = topo.addr(dst)
    return RemoteDMATransfer(dst_ids=[DstId(rid=rid, pnc=pid)], dma_engine_mask=mask, remote_sem=sem, src=ap, dst=ap)


def helper_program(g, core, T, topo, R):
    S = T.sem
    for r in range(N):
        for h in range(2):
            if R[r]["helper"][h] != core:
                continue
            m_off, m_rest, _m_all = masks_out(topo, R[r])
            n1 = count(m_off if h == 0 else m_rest)
            n2s = count(m_off if h == 0 else split(m_rest)[0])
            n2c = count(split(m_off if h == 0 else m_rest)[0])
            f0, f1 = R[r]["far"]
            m = topo.mask(core, f0)
            ma, mb = split(m)
            c2, p2 = views(T, r, W2P[h])
            p1 = views(T, r, W1P[h])[1]
            t0, t1 = 2 * h, 2 * h + 1
            sp, sb = S["p%d%d" % (r, h)], S["b%d" % r]
            g.wait_ge(S.r2s, n2s)
            g.remote_dma_fused([transfer(topo, f0, ma, sb, p2), transfer(topo, f1, mb, sb, p2)], local_sem=S.sent)
            g.wait_ge(S.rs, n1)
            g.remote_dma_fused([transfer(topo, f0, ma, sp, p1), transfer(topo, f1, mb, sp, p1)], local_sem=S.sent)
            g.wait_ge(S.rc0, n1)
            g.remote_dma_fused([transfer(topo, f0, m, S["a%d%d" % (r, t0)], tile_codes(T, r, t0))], local_sem=S.sent)
            g.wait_ge(S.rc1, n1)
            g.remote_dma_fused([transfer(topo, f0, m, S["a%d%d" % (r, t1)], tile_codes(T, r, t1))], local_sem=S.sent)
            g.remote_dma_fused([transfer(topo, f1, m, S["a%d%d" % (r, t0)], tile_codes(T, r, t0))], local_sem=S.sent)
            g.remote_dma_fused([transfer(topo, f1, m, S["a%d%d" % (r, t1)], tile_codes(T, r, t1))], local_sem=S.sent)
            g.wait_ge(S.r2c, n2c)
            g.remote_dma_fused([transfer(topo, f0, ma, sb, c2), transfer(topo, f1, mb, sb, c2)], local_sem=S.sent)
            g.wait_ge(S.sent, 3 * (count(ma) + count(mb)) + 4 * count(m))


def rank_program(g, core, T, topo):
    R = roads(T, topo)
    rank = T.rank_of(core)
    if rank is None:
        helper_program(g, core, T, topo, R)
        return
    me = R[rank]
    S = T.sem
    te, ve, se, sy = g.tensor, g.vector, g.scalar, g.sync
    lo = rank * PK

    se.dma_start(T.w2b[:], T.w2[:]).then_inc(S.l_w2, 16)
    sy.dma_start(T.w1b[:, 0:1024], T.w1[:, 0:1024]).then_inc(S.l_w1a, 16)
    sy.dma_start(T.xb[:, 0:1024], T.x[:, 0:1024]).then_inc(S.l_xa, 16)
    se.dma_start(T.w1b[:, 1024:2048], T.w1[:, 1024:2048]).then_inc(S.l_w1b, 16)
    sy.dma_start(T.xb[:, 1024:2048], T.x[:, 1024:2048]).then_inc(S.l_xb, 16)

    ve.wait_ge(S.l_w2, 16)
    ve.quantize_mx(T.wq[:, lo + W2C:lo + W2C + 128], T.ws[:, lo + W2C:lo + W2C + 128], T.w2b[:]).then_inc(S.q_w2, 1)
    ve.wait_ge(S.l_w1a, 16)
    ve.quantize_mx(T.wq[:, lo:lo + 256], T.ws[:, lo:lo + 256], T.w1b[:, 0:1024]).then_inc(S.q_w1a, 1)
    ve.wait_ge(S.l_xa, 16)
    ve.quantize_mx(T.xq[:, 0:256], T.xs[:, 0:256], T.xb[:, 0:1024]).then_inc(S.q_xa, 1)
    ve.wait_ge(S.l_w1b, 16)
    ve.quantize_mx(T.wq[:, lo + 384:lo + 640], T.ws[:, lo + 384:lo + 640], T.w1b[:, 1024:2048]).then_inc(S.q_w1b, 1)
    ve.wait_ge(S.l_xb, 16)
    ve.quantize_mx(T.xq[:, 256:512], T.xs[:, 256:512], T.xb[:, 1024:2048]).then_inc(S.q_xb, 1)

    hb, ha = me["helper"]
    near = me["near"]
    m_off, m_rest, _m_all = masks_out(topo, me)
    oa, ob = split(m_off)
    ra, rb = split(m_rest)
    c2a, p2a = views(T, rank, W2P[0])
    c2b, p2b = views(T, rank, W2P[1])
    p1a = views(T, rank, W1P[0])[1]
    p1b = views(T, rank, W1P[1])[1]
    b2 = S["b%d" % rank]

    def send_tile(t, hc, m_h, m_n):
        cc = tile_codes(T, rank, t)
        g.remote_dma_fused([transfer(topo, hc, m_h, S["rc%d" % (t % 2)], cc),
                            transfer(topo, near, m_n, S["a%d%d" % (rank, t)], cc)], local_sem=S.sent)

    g.wait_ge(S.q_w2, 1)
    g.remote_dma_fused([transfer(topo, hb, m_off, S.r2s, p2a), transfer(topo, ha, ra, S.r2s, p2b)], local_sem=S.sent)
    g.wait_ge(S.q_w1a, 1)
    g.remote_dma_fused([transfer(topo, hb, m_off, S.rs, p1a),
                        transfer(topo, near, m_rest, S["p%d0" % rank], p1a)], local_sem=S.sent)
    send_tile(0, hb, m_off, m_rest)
    send_tile(1, hb, m_off, m_rest)
    g.wait_ge(S.q_w1b, 1)
    g.remote_dma_fused([transfer(topo, ha, m_rest, S.rs, p1b),
                        transfer(topo, near, m_off, S["p%d1" % rank], p1b)], local_sem=S.sent)
    send_tile(2, ha, m_rest, m_off)
    send_tile(3, ha, m_rest, m_off)
    g.remote_dma_fused([transfer(topo, hb, oa, S.r2c, c2a), transfer(topo, ha, ra, S.r2c, c2b),
                        transfer(topo, near, ob, b2, c2a), transfer(topo, near, rb, b2, c2b)], local_sem=S.sent)
    g.remote_dma_fused([transfer(topo, near, ra, b2, p2a), transfer(topo, near, rb, b2, p2b)], local_sem=S.sent)
    g.wait_ge(S.sent, count(m_off) + count(ra) + 7 * (count(m_off) + count(m_rest)) + count(m_rest))

    def need(r, t):
        part = t // 2
        if r == rank:
            return [(("q_w1a", "q_w1b", "q_w2")[part], 1)]
        o = R[r]
        if o["near"] == core:
            off, rest, _full = masks_out(topo, o)
            if part == 2:
                return [("b%d" % r, count(split(off)[1]) + count(split(rest)[1]) + count(rest))]
            n = count(rest if part == 0 else off)
            return [("p%d%d" % (r, part), n), ("a%d%d" % (r, t), n)]
        i = o["far"].index(core)
        if part < 2:
            mh = topo.mask(o["helper"][part], core)
            return [("p%d%d" % (r, part), count(split(mh)[i])), ("a%d%d" % (r, t), count(mh))]
        return [("b%d" % r, sum(2 * count(split(topo.mask(hc, core))[i]) for hc in o["helper"]))]

    seen = set()

    def te_wait(pairs):
        for p in pairs:
            if p not in seen:
                seen.add(p)
                te.wait_ge(S[p[0]], p[1])

    cores = list(T.cores)
    order = [rank, cores.index(near)] + [cores.index(c) for c in me["far"]]
    zn = [0]
    unit_z = {}
    yn = [0, 0]

    def z_step(k, t, halves, on_scalar):
        r, z = order[k], zn[0]
        zn[0] += 1
        bank, use = z % NZ, z // NZ
        w = r * PK + tcol(t)
        c0, c1 = halves[0] * HT, (halves[-1] + 1) * HT
        te_wait(need(r, t) + [("q_xb" if s else "q_xa", 1) for s in halves])
        if use:
            te.wait_ge(S["e%d" % bank], use)
        zp = T.ps[:, bank * 512:bank * 512 + c1 - c0]
        te.matmul_mx(zp, T.wq[:, w:w + 128], T.ws[:, w:w + 128], T.xq[:, c0:c1], T.xs[:, c0:c1],
                     True, True).then_inc(S["z%d" % bank], 1)
        hv = T.h[:, 4 * (k * NT + c0) + t:4 * (k * NT + c1):4]
        if on_scalar:
            se.wait_ge(S["z%d" % bank], use + 1)
            se.activation(hv, zp, ActivationFunctionType.Relu, scale=C).then_inc(S["e%d" % bank], 1)
        else:
            ve.wait_ge(S["z%d" % bank], use + 1)
            ve.tensor_scalar(hv, zp, 0.0, C, AluOpType.max, AluOpType.mult).then_inc(S["e%d" % bank], 1)
        for s in halves:
            u = 2 * k + s
            unit_z.setdefault(u, []).append((bank, use + 1))
            if len(unit_z[u]) == 4:
                for b, n in unit_z[u]:
                    ve.wait_ge(S["e%d" % b], n)
                ve.quantize_mx(T.hq[:, u * HT:(u + 1) * HT], T.hs[:, u * HT:(u + 1) * HT],
                               T.h[:, u * 4 * HT:(u + 1) * 4 * HT]).then_inc(S["hq%d" % u], 1)

    def y_step(k, s):
        r, u = order[k], 2 * k + s
        w = r * PK + W2C
        te_wait(need(r, 4) + [("hq%d" % u, 1)])
        yn[s] += 1
        te.matmul_mx(T.ps[:, (NZ + s) * 512:(NZ + s) * 512 + HT], T.wq[:, w:w + 128], T.ws[:, w:w + 128],
                     T.hq[:, u * HT:(u + 1) * HT], T.hs[:, u * HT:(u + 1) * HT],
                     yn[s] == 1, yn[s] == N).then_inc(S["y%d" % s], 1)

    def owner(k, tiles, after_two=()):
        z_step(k, tiles[0], (0, 1), True)
        z_step(k, tiles[1], (0, 1), False)
        for kk, s in after_two:
            y_step(kk, s)
        z_step(k, tiles[2], (0, 1), True)
        z_step(k, tiles[3], (0,), False)
        z_step(k, tiles[3], (1,), True)

    for t in range(4):
        z_step(0, t, (0,), True)
    for t in range(4):
        z_step(0, t, (1,), t % 2 == 1)
    owner(1, (0, 1, 2, 3))
    y_step(0, 0)
    y_step(0, 1)
    y_step(1, 0)
    owner(2, (0, 2, 1, 3), after_two=[(1, 1)])
    owner(3, (0, 2, 1, 3))
    y_step(2, 0)
    y_step(2, 1)
    y_step(3, 0)
    y_step(3, 1)

    se.wait_ge(S.y0, N)
    se.activation(T.yo[:, 0:HT], T.ps[:, NZ * 512:NZ * 512 + HT], ActivationFunctionType.Copy).then_inc(S.cp0, 1)
    sy.wait_ge(S.cp0, 1)
    sy.dma_start(T.y[:, 0:HT], T.yo[:, 0:HT]).then_inc(S.st0, 16)
    ve.wait_ge(S.y1, N)
    ve.tensor_copy(T.yo[:, HT:2 * HT], T.ps[:, (NZ + 1) * 512:(NZ + 1) * 512 + HT]).then_inc(S.cp1, 1)
    se.wait_ge(S.cp1, 1)
    se.dma_start(T.y[:, HT:2 * HT], T.yo[:, HT:2 * HT]).then_inc(S.st1, 16)
    sy.wait_ge(S.st0, 16)
    se.wait_ge(S.st1, 16)
